import numpy as np
import ml_dtypes


def mxq(x, axis, fmt="e4m3"):
    dtype, down = {"e4m3": (ml_dtypes.float8_e4m3fn, 7), "e5m2": (ml_dtypes.float8_e5m2, 14)}[fmt]
    v = np.moveaxis(np.asarray(x, np.float32).astype(ml_dtypes.bfloat16).astype(np.float64), axis, -1)
    blocks = v.reshape(v.shape[:-1] + (-1, 32))
    amax = np.abs(blocks).max(-1, keepdims=True)
    byte = np.maximum(np.where(amax > 0, np.frexp(amax)[1] - 1 + 127, 0) - down, 1)
    scale = np.exp2(byte - 127.0)
    codes = (blocks / scale).astype(np.float32).astype(dtype).astype(np.float64)
    return np.moveaxis((codes * scale).reshape(v.shape), -1, axis)


WIDE = False


def mx_kscale(k):
    if not WIDE:
        return np.ones(k)
    levels = np.array([10, -10, 5, -5, 0])
    if k % 512:
        return np.exp2(np.random.permutation(np.resize(levels, k // 32))).repeat(32)
    a = np.empty((k // 512, 16))
    for p in range(k // 512):
        a[p, :8] = np.random.permutation(np.resize(levels, 8))
        for g in range(8):
            far = levels[np.abs(levels - a[p, g]) >= 10]
            a[p, g + 8] = far[np.random.randint(len(far))]
    return np.exp2(a.ravel()).repeat(32)


BF16 = ml_dtypes.bfloat16


def bf(x):
    return np.asarray(x, np.float32).astype(BF16)


def f64(x):
    return np.asarray(x).astype(np.float64)


N, M, D, F = 1024, 1024, 512, 1024


def hidden_sensitivity(inp_q, w, b, v):
    t = np.tanh((inp_q @ mxq(f64(w), 0, "e4m3")) + f64(b))
    return (1.0 - t * t) * f64(v)


def draw0():
    s, u = mx_kscale(D), mx_kscale(F)
    return {
        "x": bf(np.random.standard_normal((N, D)) * s),
        "y": bf(np.random.standard_normal((M, D)) / s),
        "wa": bf(np.random.standard_normal((D, F)) / np.sqrt(D) / s[:, None]),
        "wb": bf(np.random.standard_normal((D, F)) / np.sqrt(D) * s[:, None]),
        "b": bf(0.5 * np.random.standard_normal(F)),
        "va": bf(np.random.standard_normal(F) * u),
        "vb": bf(np.random.standard_normal(F) / u),
    }


def core(x, y, wa, wb, b, va, vb):
    d = x.shape[1]
    f = wa.shape[1]
    xq = mxq(f64(x), 1, "e4m3")
    yq = mxq(f64(y), 1, "e4m3")
    da = hidden_sensitivity(xq, wa, b, va)
    db = hidden_sensitivity(yq, wb, b, vb)
    gram = (mxq(da, 1, "e4m3") @ mxq(db, 1, "e4m3").T) / np.sqrt(f)
    base = (xq @ yq.T) / np.sqrt(d)
    return base * gram


def e4m3fn_bytes(y):
    return np.clip(np.asarray(y, np.float64), -448.0, 448.0).astype(np.float32).astype(ml_dtypes.float8_e4m3fn).view(np.uint8)


def e4m3fn_values(b):
    return np.asarray(b, np.uint8).view(ml_dtypes.float8_e4m3fn).astype(np.float64)


def setup_inputs():
    d = draw0()
    x0 = np.asarray(d['y']).astype(np.float64)
    s = (np.max(np.abs(x0), axis=(0,), keepdims=True) / 448.0).astype(np.float32)
    out = {}
    for k, v in d.items():
        if k == 'y':
            out['y_bytes'] = e4m3fn_bytes(x0 / s.astype(np.float64))
            out['y_scale'] = s
        else:
            out[k] = v
    return out


def reference(x, y_bytes, y_scale, wa, wb, b, va, vb):
    return core(x, e4m3fn_values(y_bytes) * y_scale.astype(np.float64), wa, wb, b, va, vb)

@@ -1,0 +1,409 @@
+import math
+from contextlib import ExitStack
+
+import concourse.mybir as mybir
+from concourse.masks import make_identity
+
+N, M, D, F = 1024, 1024, 512, 1024
+FLOPS = 2 * N * D * F + 2 * M * D * F + 2 * N * M * D + 2 * N * M * F
+
+F32 = mybir.dt.float32
+BF16 = mybir.dt.bfloat16
+U32 = mybir.dt.uint32
+U8 = mybir.dt.uint8
+FP8 = mybir.dt.float8_e4m3fn
+FP8X4 = mybir.dt.float8_e4m3fn_x4
+ACT = mybir.ActivationFunctionType
+ALU = mybir.AluOpType
+
+P = 128
+PACK = 4
+K_PASS = P * PACK
+BANK = 512
+BLOCK = 256
+BLOCKS = N // BLOCK
+PASSES = F // K_PASS
+PAD = 16
+BANKS = {"pre": 4, "for_s": 1, "for_v": 3}
+
+
+def tile_twotimehiddentangentkernel_kernel(tc, x, y_bytes, y_scale, wa, wb, b, va, vb, out):
+    nc = tc.nc
+    with ExitStack() as ctx:
+        keep = ctx.enter_context(tc.tile_pool(name="keep", bufs=1))
+        work = ctx.enter_context(tc.tile_pool(name="work", bufs=4))
+        psum = ctx.enter_context(tc.psum_pool(name="psum", bufs=4))
+
+        ident = keep.tile([P, P], F32, name="ident")
+        make_identity(nc, ident[:])
+
+        ctx.enter_context(tc.manual_schedule())
+
+        def mx_tiles(name, width):
+            codes = keep.tile([P, width], U32, name=name + "_codes", align_bytes=64)
+            scales = keep.tile([P, width], U8, name=name + "_scales", align_bytes=64)
+            return codes, scales
+
+        def quantize(dst, col0, grouped):
+            width = grouped.shape[1] // PACK
+            nc.vector.quantize_mx(
+                out=dst[0][:, col0 : col0 + width].bitcast(FP8X4),
+                scales=dst[1][:, col0 : col0 + width],
+                in_=grouped,
+            )
+
+        def mx_matmul(acc, lhs, lhs0, rhs, rhs0, width, start, stop):
+            nc.tensor.matmul_mx(
+                out=acc,
+                lhsT=lhs[0][:, lhs0 : lhs0 + P].bitcast(FP8X4),
+                lhsT_scale=lhs[1][:, lhs0 : lhs0 + P],
+                rhs=rhs[0][:, rhs0 : rhs0 + width].bitcast(FP8X4),
+                rhs_scale=rhs[1][:, rhs0 : rhs0 + width],
+                start=start,
+                stop=stop,
+            )
+
+        tok_mx = {"a": mx_tiles("x", N), "b": mx_tiles("y", M)}
+        w_mx = {(s, g): mx_tiles("w%s%d" % (s, g), K_PASS) for s in "ab" for g in range(PASSES)}
+        d_mx = {(s, g): mx_tiles("d%s%d" % (s, g), N) for s in "ab" for g in range(PASSES)}
+        weights = {"a": wa, "b": wb}
+        gains = {"a": va, "b": vb}
+        x_raw, y_raw, w_raw, gain_raw, neg_gain = {}, {}, {}, {}, {}
+        tok_bf, tok_bank, grouped, squares, base_sb = {}, {}, {}, {}, {}
+        pre_banks, tanhs, base_banks, gram_banks = {}, {}, {}, {}
+
+        def load_y(blk):
+            t = keep.tile([P, 2, D], U8, name="ybytes%d" % blk)
+            nc.sync.dma_start(out=t[:], in_=y_bytes[blk * BLOCK : (blk + 1) * BLOCK, :].rearrange("(a p) k -> p a k", p=P))
+            y_raw[blk] = t
+
+        def load_x(blk):
+            t = keep.tile([P, 2, D], BF16, name="xrows%d" % blk)
+            nc.sync.dma_start(out=t[:], in_=x[blk * BLOCK : (blk + 1) * BLOCK, :].rearrange("(p a) k -> p a k", a=2))
+            tok_bf["a", blk] = t
+
+        def load_w(s, g):
+            t = keep.tile([P, PACK, K_PASS], BF16, name="wraw%s%d" % (s, g))
+            nc.sync.dma_start(
+                out=t[:], in_=weights[s][:, g * K_PASS : (g + 1) * K_PASS].rearrange("(p k) c -> p k c", k=PACK)
+            )
+            w_raw[s, g] = t
+
+        def load_channels(vec, name):
+            t = keep.tile([P, PASSES, PAD], BF16, name=name)
+            nc.sync.dma_start(out=t[:, :, 0:PACK], in_=vec.rearrange("(g p j) -> p g j", p=P, j=PACK))
+            return t
+
+        load_x(0)
+        load_w("a", 0)
+        load_y(0)
+        bias = load_channels(b, "bias")
+        load_x(1)
+        gain_raw["a"] = load_channels(va, "va_raw")
+        load_y(1)
+        load_w("a", 1)
+        y_gain = keep.tile([P, PACK], F32, name="y_gain")
+        nc.sync.dma_start(out=y_gain[:], in_=y_scale.rearrange("o (p t) -> p (o t)", t=PACK))
+        load_w("b", 0)
+        gain_raw["b"] = load_channels(vb, "vb_raw")
+        load_y(2)
+        load_y(3)
+        load_w("b", 1)
+        load_x(2)
+        load_x(3)
+
+        def negate_gain(s):
+            t = keep.tile([P, PASSES, PACK], F32, name="neg_v%s" % s)
+            nc.scalar.activation(out=t[:], in_=gain_raw[s][:, :, 0:PACK], func=ACT.Copy, scale=-1.0)
+            neg_gain[s] = t
+
+        def widen_y(blk, engine_copy):
+            t = keep.tile([P, 2, D], BF16, name="ywide%d" % blk)
+            engine_copy(out=t[:], in_=y_raw[blk][:].bitcast(FP8))
+            tok_bf["b", blk] = t
+
+        def turn(s, blk):
+            tag = "for_v" if s == "b" else "for_s"
+            bank = psum.tile([P, 2, BLOCK], F32, name="turned", tag=tag, bufs=BANKS[tag])
+            for a in range(2):
+                words = tok_bf[s, blk][:, a, :].bitcast(F32)
+                for u in range(2):
+                    nc.tensor.transpose(bank[:, u, a * P : (a + 1) * P], words[:, u : D // 2 : 2], ident[:])
+            tok_bank[s, blk] = bank
+
+        def gather_x(blk, engine_copy):
+            t = keep.tile([P, BLOCK * PACK], BF16, name="xgrouped%d" % blk, align_bytes=64)
+            engine_copy(
+                out=t[:].bitcast(F32).rearrange("p (n u) -> p n u", u=2),
+                in_=tok_bank["a", blk][:].rearrange("p u n -> p n u"),
+            )
+            grouped["a", blk] = t
+
+        def scale_y(blk):
+            t = keep.tile([P, BLOCK * PACK], BF16, name="ygrouped%d" % blk, align_bytes=64)
+            halves = tok_bank["b", blk][:].rearrange("p u n -> p (u n)").bitcast(BF16)
+            nc.vector.tensor_tensor(
+                out=t[:].rearrange("p (n u e) -> p n u e", u=2, e=2),
+                in0=halves.rearrange("p (u n e) -> p n u e", u=2, e=2),
+                in1=y_gain[:].rearrange("p (u e) -> p u e", e=2).unsqueeze(1).to_broadcast([P, BLOCK, 2, 2]),
+                op=ALU.mult,
+            )
+            grouped["b", blk] = t
+
+        def quantize_tokens(s, blk):
+            quantize(tok_mx[s], blk * BLOCK, grouped[s, blk][:])
+
+        def group_w(s, g, copies):
+            share = PACK // len(copies)
+            src = w_raw[s, g][:].rearrange("p k (h l j) -> p h j l k", l=2, j=PACK)
+            for i, engine_copy in enumerate(copies):
+                t = keep.tile([P, share * K_PASS], BF16, name="wgrouped%s%d_%d" % (s, g, i), align_bytes=64)
+                engine_copy(
+                    out=t[:].rearrange("p (j h l k) -> p h j l k", j=share, l=2, k=PACK),
+                    in_=src[:, :, i * share : (i + 1) * share],
+                )
+                grouped["w", s, g, i] = t
+
+        def quantize_w(s, g, part=0, parts=1):
+            quantize(w_mx[s, g], part * K_PASS // parts, grouped["w", s, g, part][:])
+
+        def preact(s, g, col0, width):
+            per_bank = BANK // width
+            views = []
+            for j0 in range(0, PACK, per_bank):
+                bank = psum.tile([P, per_bank, width], F32, name="pre", tag="pre", bufs=BANKS["pre"])
+                for i in range(min(per_bank, PACK)):
+                    mx_matmul(bank[:, i, :], w_mx[s, g], (j0 + i) * P, tok_mx[s], col0, width, True, True)
+                    views.append(bank[:, i, :])
+            pre_banks[s, g, col0] = views
+
+        def tanh(s, g, col0, width):
+            planes = work.tile([P, PACK, width], F32, name="tanh_planes", tag="tanh_planes", bufs=2)
+            for j in range(PACK):
+                nc.scalar.activation(
+                    out=planes[:, j, :], in_=pre_banks[s, g, col0][j], func=ACT.Tanh, bias=bias[:, g, j : j + 1]
+                )
+            tanhs[s, g, col0] = planes
+
+        def square(s, g, col0, width):
+            sq = work.tile([P, width * PACK], F32, name="squares", tag="squares")
+            nc.scalar.activation(
+                out=sq[:].rearrange("p (c i j) -> p c j i", i=2, j=PACK),
+                in_=tanhs[s, g, col0][:].rearrange("p j (c i) -> p c j i", i=2),
+                func=ACT.Square,
+            )
+            squares[s, g, col0] = sq
+
+        def derive(s, g, col0, width):
+            t = work.tile([P, width * PACK], BF16, name="dgrouped", tag="dgrouped", bufs=3, align_bytes=64)
+            nc.vector.scalar_tensor_tensor(
+                out=t[:].rearrange("p (n j) -> p n j", j=PACK),
+                in0=squares[s, g, col0][:].rearrange("p (n j) -> p n j", j=PACK),
+                scalar=1.0,
+                in1=neg_gain[s][:, g, :].unsqueeze(1).to_broadcast([P, width, PACK]),
+                op0=ALU.subtract,
+                op1=ALU.mult,
+            )
+            grouped["d", s, g, col0] = t
+
+        def quantize_d(s, g, col0, width):
+            quantize(d_mx[s, g], col0, grouped["d", s, g, col0][:])
+
+        def base_matmul(tile, half, tag):
+            bank = psum.tile([P, BANK], F32, name="base_acc", tag=tag, bufs=BANKS[tag])
+            mx_matmul(bank[:], tok_mx["a"], tile * P, tok_mx["b"], half * BANK, BANK, True, True)
+            base_banks[tile, half] = bank
+
+        def base_on_s(tile, half):
+            t = keep.tile([P, BANK], F32, name="base%d_%d" % (tile, half))
+            nc.scalar.activation(out=t[:], in_=base_banks[tile, half][:], func=ACT.Copy, scale=1.0 / math.sqrt(D))
+            base_sb[tile, half] = t
+
+        def base_on_v(tile, half):
+            t = keep.tile([P, BANK], F32, name="base%d_%d" % (tile, half))
+            nc.vector.tensor_scalar(
+                out=t[:], in0=base_banks[tile, half][:], scalar1=1.0 / math.sqrt(D), scalar2=None, op0=ALU.mult
+            )
+            base_sb[tile, half] = t
+
+        def gram(tile, half):
+            bank = psum.tile([P, BANK], F32, name="gram_acc", tag="for_v", bufs=BANKS["for_v"])
+            for g in range(PASSES):
+                mx_matmul(bank[:], d_mx["a", g], tile * P, d_mx["b", g], half * BANK, BANK, g == 0, g == PASSES - 1)
+            gram_banks[tile, half] = bank
+
+        def finish(tile, half):
+            t = keep.tile([P, BANK], F32, name="out%d_%d" % (tile, half))
+            nc.vector.scalar_tensor_tensor(
+                out=t[:],
+                in0=gram_banks[tile, half][:],
+                scalar=1.0 / math.sqrt(F),
+                in1=base_sb[tile, half][:],
+                op0=ALU.mult,
+                op1=ALU.mult,
+            )
+            blk, a = divmod(tile, 2)
+            rows = out[blk * BLOCK : (blk + 1) * BLOCK, half * BANK : (half + 1) * BANK]
+            nc.sync.dma_start(out=rows.rearrange("(p a) m -> p a m", a=2)[:, a, :], in_=t[:])
+
+        on_s, on_v = nc.scalar.copy, nc.vector.tensor_copy
+        u = [("a", 0, 0, 256), ("a", 0, 256, 256), ("a", 1, 0, 512), ("b", 0, 0, 512), ("b", 1, 0, 512),
+             ("b", 0, 512, 512), ("b", 1, 512, 512), ("a", 0, 512, 512), ("a", 1, 512, 256), ("a", 1, 768, 128), ("a", 1, 896, 128)]
+        turn("a", 0)
+        gather_x(0, on_s)
+        group_w("a", 0, [on_v, on_s])
+        quantize_tokens("a", 0)
+        quantize_w("a", 0, 0, 2)
+        turn("a", 1)
+        widen_y(0, on_v)
+        quantize_w("a", 0, 1, 2)
+        gather_x(1, on_s)
+        preact(*u[0])
+        widen_y(1, on_v)
+        quantize_tokens("a", 1)
+        turn("b", 0)
+        tanh(*u[0])
+        preact(*u[1])
+        turn("b", 1)
+        group_w("a", 1, [on_v])
+        scale_y(0)
+        quantize_w("a", 1)
+        negate_gain("a")
+        square(*u[0])
+        tanh(*u[1])
+        preact(*u[2])
+        scale_y(1)
+        quantize_tokens("b", 0)
+        group_w("b", 0, [on_v])
+        quantize_tokens("b", 1)
+        base_matmul(0, 0, "for_s")
+        negate_gain("b")
+        square(*u[1])
+        tanh(*u[2])
+        derive(*u[0])
+        quantize_w("b", 0)
+        base_on_s(0, 0)
+        preact(*u[3])
+        base_matmul(1, 0, "for_s")
+        group_w("b", 1, [on_v])
+        quantize_d(*u[0])
+        derive(*u[1])
+        quantize_w("b", 1)
+        quantize_d(*u[1])
+        widen_y(2, on_v)
+        widen_y(3, on_v)
+        square(*u[2])
+        tanh(*u[3])
+        base_on_s(1, 0)
+        preact(*u[4])
+        turn("b", 2)
+        turn("b", 3)
+        turn("a", 2)
+        base_matmul(2, 0, "for_v")
+        derive(*u[2])
+        scale_y(2)
+        base_matmul(3, 0, "for_v")
+        quantize_d(*u[2])
+        scale_y(3)
+        quantize_tokens("b", 2)
+        square(*u[3])
+        tanh(*u[4])
+        gather_x(2, on_s)
+        turn("a", 3)
+        quantize_tokens("b", 3)
+        preact(*u[5])
+        derive(*u[3])
+        quantize_tokens("a", 2)
+        quantize_d(*u[3])
+        square(*u[4])
+        tanh(*u[5])
+        gather_x(3, on_s)
+        preact(*u[6])
+        base_matmul(0, 1, "for_s")
+        derive(*u[4])
+        base_on_v(2, 0)
+        quantize_d(*u[4])
+        gram(0, 0)
+        gram(1, 0)
+        base_on_v(3, 0)
+        quantize_tokens("a", 3)
+        gram(2, 0)
+        square(*u[5])
+        base_on_s(0, 1)
+        base_matmul(1, 1, "for_s")
+        finish(0, 0)
+        gram(3, 0)
+        finish(1, 0)
+        base_matmul(2, 1, "for_v")
+        tanh(*u[6])
+        base_on_s(1, 1)
+        preact(*u[7])
+        base_matmul(4, 0, "for_s")
+        derive(*u[5])
+        finish(2, 0)
+        base_matmul(3, 1, "for_v")
+        quantize_d(*u[5])
+        finish(3, 0)
+        base_matmul(5, 0, "for_v")
+        base_on_v(2, 1)
+        square(*u[6])
+        base_on_s(4, 0)
+        base_matmul(4, 1, "for_s")
+        tanh(*u[7])
+        base_on_s(4, 1)
+        preact(*u[8])
+        base_matmul(5, 1, "for_s")
+        derive(*u[6])
+        base_on_v(3, 1)
+        quantize_d(*u[6])
+        gram(0, 1)
+        gram(1, 1)
+        base_on_v(5, 0)
+        gram(2, 1)
+        finish(0, 1)
+        gram(3, 1)
+        finish(1, 1)
+        square(*u[7])
+        base_on_s(5, 1)
+        preact(*u[9])
+        base_matmul(6, 0, "for_s")
+        tanh(*u[8])
+        base_on_s(6, 0)
+        preact(*u[10])
+        base_matmul(6, 1, "for_s")
+        derive(*u[7])
+        finish(2, 1)
+        quantize_d(*u[7])
+        finish(3, 1)
+        square(*u[8])
+        base_on_s(6, 1)
+        base_matmul(7, 0, "for_s")
+        tanh(*u[9])
+        base_on_s(7, 0)
+        base_matmul(7, 1, "for_s")
+        derive(*u[8])
+        square(*u[9])
+        tanh(*u[10])
+        base_on_s(7, 1)
+        square(*u[10])
+        quantize_d(*u[8])
+        gram(4, 0)
+        gram(4, 1)
+        gram(5, 0)
+        derive(*u[9])
+        finish(4, 0)
+        gram(5, 1)
+        quantize_d(*u[9])
+        finish(4, 1)
+        gram(6, 0)
+        derive(*u[10])
+        finish(5, 0)
+        gram(6, 1)
+        quantize_d(*u[10])
+        finish(5, 1)
+        gram(7, 0)
+        finish(6, 0)
+        gram(7, 1)
+        finish(6, 1)
+        finish(7, 0)
+        finish(7, 1)

@@ -113,8 +113,9 @@ def tile_twotimehiddentangentkernel_kernel(tc, x, y_bytes, y_scale, wa, wb, b, v
         load_x(3)
 
         def negate_gain(s):
-            t = keep.tile([P, PASSES, PACK], F32, name="neg_v%s" % s)
-            nc.scalar.activation(out=t[:], in_=gain_raw[s][:, :, 0:PACK], func=ACT.Copy, scale=-1.0)
+            t = keep.tile([P, PASSES, PACK, 2], F32, name="neg_v%s" % s)
+            twice = gain_raw[s][:, :, 0:PACK].unsqueeze(3).to_broadcast([P, PASSES, PACK, 2])
+            nc.scalar.activation(out=t[:], in_=twice, func=ACT.Copy, scale=-1.0)
             neg_gain[s] = t
 
         def widen_y(blk, engine_copy):
@@ -181,14 +182,17 @@ def tile_twotimehiddentangentkernel_kernel(tc, x, y_bytes, y_scale, wa, wb, b, v
             planes = work.tile([P, PACK, width], F32, name="tanh_planes", tag="tanh_planes", bufs=2)
             for j in range(PACK):
                 nc.scalar.activation(
-                    out=planes[:, j, :], in_=pre_banks[s, g, col0][j], func=ACT.Tanh, bias=bias[:, g, j : j + 1]
+                    out=planes[:, j, :].rearrange("p (c i) -> p c i", i=2),
+                    in_=pre_banks[s, g, col0][j].rearrange("p (i c) -> p c i", i=2),
+                    func=ACT.Tanh,
+                    bias=bias[:, g, j : j + 1],
                 )
             tanhs[s, g, col0] = planes
 
         def square(s, g, col0, width):
             sq = work.tile([P, width * PACK], F32, name="squares", tag="squares")
             nc.scalar.activation(
-                out=sq[:].rearrange("p (c i j) -> p c j i", i=2, j=PACK),
+                out=sq[:].rearrange("p (c j i) -> p c j i", i=2, j=PACK),
                 in_=tanhs[s, g, col0][:].rearrange("p j (c i) -> p c j i", i=2),
                 func=ACT.Square,
             )
@@ -197,10 +201,10 @@ def tile_twotimehiddentangentkernel_kernel(tc, x, y_bytes, y_scale, wa, wb, b, v
         def derive(s, g, col0, width):
             t = work.tile([P, width * PACK], BF16, name="dgrouped", tag="dgrouped", bufs=3, align_bytes=64)
             nc.vector.scalar_tensor_tensor(
-                out=t[:].rearrange("p (n j) -> p n j", j=PACK),
-                in0=squares[s, g, col0][:].rearrange("p (n j) -> p n j", j=PACK),
+                out=t[:].rearrange("p (i c j) -> p c j i", i=2, j=PACK),
+                in0=squares[s, g, col0][:].rearrange("p (c j i) -> p c j i", i=2, j=PACK),
                 scalar=1.0,
-                in1=neg_gain[s][:, g, :].unsqueeze(1).to_broadcast([P, width, PACK]),
+                in1=neg_gain[s][:, g].unsqueeze(1).to_broadcast([P, width // 2, PACK, 2]),
                 op0=ALU.subtract,
                 op1=ALU.mult,
             )
@@ -248,7 +252,8 @@ def tile_twotimehiddentangentkernel_kernel(tc, x, y_bytes, y_scale, wa, wb, b, v
 
         on_s, on_v = nc.scalar.copy, nc.vector.tensor_copy
         u = [("a", 0, 0, 256), ("a", 0, 256, 256), ("a", 1, 0, 512), ("b", 0, 0, 512), ("b", 1, 0, 512),
-             ("b", 0, 512, 512), ("b", 1, 512, 512), ("a", 0, 512, 512), ("a", 1, 512, 256), ("a", 1, 768, 128), ("a", 1, 896, 128)]
+             ("b", 0, 512, 512), ("b", 1, 512, 512), ("a", 0, 512, 256), ("a", 1, 512, 256), ("a", 0, 768, 256),
+             ("a", 1, 768, 128), ("a", 1, 896, 128)]
         turn("a", 0)
         gather_x(0, on_s)
         group_w("a", 0, [on_v, on_s])
@@ -339,68 +344,73 @@ def tile_twotimehiddentangentkernel_kernel(tc, x, y_bytes, y_scale, wa, wb, b, v
         base_on_s(1, 1)
         preact(*u[7])
         base_matmul(4, 0, "for_s")
+        preact(*u[8])
         derive(*u[5])
         finish(2, 0)
         base_matmul(3, 1, "for_v")
         quantize_d(*u[5])
         finish(3, 0)
-        base_matmul(5, 0, "for_v")
+        base_matmul(4, 1, "for_v")
         base_on_v(2, 1)
         square(*u[6])
-        base_on_s(4, 0)
-        base_matmul(4, 1, "for_s")
         tanh(*u[7])
-        base_on_s(4, 1)
-        preact(*u[8])
-        base_matmul(5, 1, "for_s")
+        base_on_s(4, 0)
+        base_matmul(5, 0, "for_s")
+        preact(*u[9])
         derive(*u[6])
         base_on_v(3, 1)
         quantize_d(*u[6])
         gram(0, 1)
         gram(1, 1)
-        base_on_v(5, 0)
+        base_on_v(4, 1)
         gram(2, 1)
+        square(*u[7])
+        tanh(*u[8])
+        base_on_s(5, 0)
+        base_matmul(5, 1, "for_s")
+        preact(*u[10])
+        preact(*u[11])
         finish(0, 1)
         gram(3, 1)
-        finish(1, 1)
-        square(*u[7])
-        base_on_s(5, 1)
-        preact(*u[9])
-        base_matmul(6, 0, "for_s")
-        tanh(*u[8])
-        base_on_s(6, 0)
-        preact(*u[10])
-        base_matmul(6, 1, "for_s")
         derive(*u[7])
-        finish(2, 1)
+        finish(1, 1)
         quantize_d(*u[7])
-        finish(3, 1)
+        finish(2, 1)
         square(*u[8])
-        base_on_s(6, 1)
-        base_matmul(7, 0, "for_s")
+        base_on_s(5, 1)
+        base_matmul(6, 0, "for_s")
         tanh(*u[9])
-        base_on_s(7, 0)
-        base_matmul(7, 1, "for_s")
+        base_on_s(6, 0)
+        base_matmul(6, 1, "for_s")
         derive(*u[8])
-        square(*u[9])
-        tanh(*u[10])
-        base_on_s(7, 1)
-        square(*u[10])
+        finish(3, 1)
         quantize_d(*u[8])
         gram(4, 0)
+        square(*u[9])
+        base_on_s(6, 1)
+        base_matmul(7, 0, "for_s")
         gram(4, 1)
         gram(5, 0)
+        tanh(*u[10])
+        base_on_s(7, 0)
+        base_matmul(7, 1, "for_s")
+        square(*u[10])
+        tanh(*u[11])
+        base_on_s(7, 1)
+        square(*u[11])
         derive(*u[9])
         finish(4, 0)
         gram(5, 1)
         quantize_d(*u[9])
         finish(4, 1)
-        gram(6, 0)
         derive(*u[10])
         finish(5, 0)
-        gram(6, 1)
         quantize_d(*u[10])
+        gram(6, 0)
+        gram(6, 1)
+        derive(*u[11])
         finish(5, 1)
+        quantize_d(*u[11])
         gram(7, 0)
         finish(6, 0)
         gram(7, 1)

@@ -95,12 +95,12 @@ def tile_twotimehiddentangentkernel_kernel(tc, x, y_bytes, y_scale, wa, wb, b, v
             return t
 
         load_x(0)
-        load_w("a", 0)
         load_y(0)
-        bias = load_channels(b, "bias")
+        load_w("a", 0)
         load_x(1)
-        gain_raw["a"] = load_channels(va, "va_raw")
         load_y(1)
+        bias = load_channels(b, "bias")
+        gain_raw["a"] = load_channels(va, "va_raw")
         load_w("a", 1)
         y_gain = keep.tile([P, PACK], F32, name="y_gain")
         nc.sync.dma_start(out=y_gain[:], in_=y_scale.rearrange("o (p t) -> p (o t)", t=PACK))
@@ -132,27 +132,34 @@ def tile_twotimehiddentangentkernel_kernel(tc, x, y_bytes, y_scale, wa, wb, b, v
                     nc.tensor.transpose(bank[:, u, a * P : (a + 1) * P], words[:, u : D // 2 : 2], ident[:])
             tok_bank[s, blk] = bank
 
+        def grouped_block(s, blk):
+            if (s, blk // 2) not in grouped:
+                t = keep.tile([P, 2 * BLOCK * PACK], BF16, name="grouped%s%d" % (s, blk // 2), align_bytes=64)
+                grouped[s, blk // 2] = t
+            return grouped[s, blk // 2][:, (blk % 2) * BLOCK * PACK : (blk % 2 + 1) * BLOCK * PACK]
+
         def gather_x(blk, engine_copy):
-            t = keep.tile([P, BLOCK * PACK], BF16, name="xgrouped%d" % blk, align_bytes=64)
+            t = grouped_block("a", blk)
             engine_copy(
-                out=t[:].bitcast(F32).rearrange("p (n u) -> p n u", u=2),
+                out=t.bitcast(F32).rearrange("p (n u) -> p n u", u=2),
                 in_=tok_bank["a", blk][:].rearrange("p u n -> p n u"),
             )
-            grouped["a", blk] = t
 
         def scale_y(blk):
-            t = keep.tile([P, BLOCK * PACK], BF16, name="ygrouped%d" % blk, align_bytes=64)
+            t = grouped_block("b", blk)
             halves = tok_bank["b", blk][:].rearrange("p u n -> p (u n)").bitcast(BF16)
             nc.vector.tensor_tensor(
-                out=t[:].rearrange("p (n u e) -> p n u e", u=2, e=2),
+                out=t.rearrange("p (n u e) -> p n u e", u=2, e=2),
                 in0=halves.rearrange("p (u n e) -> p n u e", u=2, e=2),
                 in1=y_gain[:].rearrange("p (u e) -> p u e", e=2).unsqueeze(1).to_broadcast([P, BLOCK, 2, 2]),
                 op=ALU.mult,
             )
-            grouped["b", blk] = t
 
         def quantize_tokens(s, blk):
-            quantize(tok_mx[s], blk * BLOCK, grouped[s, blk][:])
+            quantize(tok_mx[s], blk * BLOCK, grouped_block(s, blk))
+
+        def quantize_pair(s, pair):
+            quantize(tok_mx[s], pair * 2 * BLOCK, grouped[s, pair][:])
 
         def group_w(s, g, copies):
             share = PACK // len(copies)
@@ -236,41 +243,45 @@ def tile_twotimehiddentangentkernel_kernel(tc, x, y_bytes, y_scale, wa, wb, b, v
                 mx_matmul(bank[:], d_mx["a", g], tile * P, d_mx["b", g], half * BANK, BANK, g == 0, g == PASSES - 1)
             gram_banks[tile, half] = bank
 
-        def finish(tile, half):
-            t = keep.tile([P, BANK], F32, name="out%d_%d" % (tile, half))
-            nc.vector.scalar_tensor_tensor(
-                out=t[:],
-                in0=gram_banks[tile, half][:],
-                scalar=1.0 / math.sqrt(F),
-                in1=base_sb[tile, half][:],
-                op0=ALU.mult,
-                op1=ALU.mult,
-            )
+        def finish(tile, half, pieces=1):
             blk, a = divmod(tile, 2)
-            rows = out[blk * BLOCK : (blk + 1) * BLOCK, half * BANK : (half + 1) * BANK]
-            nc.sync.dma_start(out=rows.rearrange("(p a) m -> p a m", a=2)[:, a, :], in_=t[:])
+            width = BANK // pieces
+            for i in range(pieces):
+                cols = slice(i * width, (i + 1) * width)
+                t = keep.tile([P, width], F32, name="out%d_%d_%d" % (tile, half, i))
+                nc.vector.scalar_tensor_tensor(
+                    out=t[:],
+                    in0=gram_banks[tile, half][:, cols],
+                    scalar=1.0 / math.sqrt(F),
+                    in1=base_sb[tile, half][:, cols],
+                    op0=ALU.mult,
+                    op1=ALU.mult,
+                )
+                m0 = half * BANK + i * width
+                rows = out[blk * BLOCK : (blk + 1) * BLOCK, m0 : m0 + width]
+                nc.sync.dma_start(out=rows.rearrange("(p a) m -> p a m", a=2)[:, a, :], in_=t[:])
 
         on_s, on_v = nc.scalar.copy, nc.vector.tensor_copy
         u = [("a", 0, 0, 256), ("a", 0, 256, 256), ("a", 1, 0, 512), ("b", 0, 0, 512), ("b", 1, 0, 512),
              ("b", 0, 512, 512), ("b", 1, 512, 512), ("a", 0, 512, 256), ("a", 1, 512, 256), ("a", 0, 768, 256),
              ("a", 1, 768, 128), ("a", 1, 896, 128)]
         turn("a", 0)
+        widen_y(0, on_v)
         gather_x(0, on_s)
         group_w("a", 0, [on_v, on_s])
         quantize_tokens("a", 0)
         quantize_w("a", 0, 0, 2)
         turn("a", 1)
-        widen_y(0, on_v)
+        widen_y(1, on_v)
         quantize_w("a", 0, 1, 2)
         gather_x(1, on_s)
         preact(*u[0])
-        widen_y(1, on_v)
-        quantize_tokens("a", 1)
         turn("b", 0)
+        group_w("a", 1, [on_v])
+        quantize_tokens("a", 1)
         tanh(*u[0])
         preact(*u[1])
         turn("b", 1)
-        group_w("a", 1, [on_v])
         scale_y(0)
         quantize_w("a", 1)
         negate_gain("a")
@@ -278,9 +289,8 @@ def tile_twotimehiddentangentkernel_kernel(tc, x, y_bytes, y_scale, wa, wb, b, v
         tanh(*u[1])
         preact(*u[2])
         scale_y(1)
-        quantize_tokens("b", 0)
         group_w("b", 0, [on_v])
-        quantize_tokens("b", 1)
+        quantize_pair("b", 0)
         base_matmul(0, 0, "for_s")
         negate_gain("b")
         square(*u[1])
@@ -308,17 +318,16 @@ def tile_twotimehiddentangentkernel_kernel(tc, x, y_bytes, y_scale, wa, wb, b, v
         derive(*u[2])
         scale_y(2)
         base_matmul(3, 0, "for_v")
-        quantize_d(*u[2])
         scale_y(3)
-        quantize_tokens("b", 2)
+        quantize_d(*u[2])
+        quantize_pair("b", 1)
         square(*u[3])
         tanh(*u[4])
         gather_x(2, on_s)
         turn("a", 3)
-        quantize_tokens("b", 3)
         preact(*u[5])
         derive(*u[3])
-        quantize_tokens("a", 2)
+        base_on_v(2, 0)
         quantize_d(*u[3])
         square(*u[4])
         tanh(*u[5])
@@ -326,87 +335,86 @@ def tile_twotimehiddentangentkernel_kernel(tc, x, y_bytes, y_scale, wa, wb, b, v
         preact(*u[6])
         base_matmul(0, 1, "for_s")
         derive(*u[4])
-        base_on_v(2, 0)
+        base_on_v(3, 0)
         quantize_d(*u[4])
         gram(0, 0)
         gram(1, 0)
-        base_on_v(3, 0)
-        quantize_tokens("a", 3)
         gram(2, 0)
+        quantize_pair("a", 1)
         square(*u[5])
-        base_on_s(0, 1)
-        base_matmul(1, 1, "for_s")
         finish(0, 0)
         gram(3, 0)
         finish(1, 0)
-        base_matmul(2, 1, "for_v")
         tanh(*u[6])
-        base_on_s(1, 1)
+        base_on_s(0, 1)
         preact(*u[7])
-        base_matmul(4, 0, "for_s")
+        base_matmul(1, 1, "for_s")
         preact(*u[8])
         derive(*u[5])
         finish(2, 0)
-        base_matmul(3, 1, "for_v")
+        base_matmul(4, 0, "for_v")
         quantize_d(*u[5])
         finish(3, 0)
-        base_matmul(4, 1, "for_v")
-        base_on_v(2, 1)
         square(*u[6])
         tanh(*u[7])
-        base_on_s(4, 0)
-        base_matmul(5, 0, "for_s")
+        base_on_s(1, 1)
+        base_matmul(2, 1, "for_s")
         preact(*u[9])
         derive(*u[6])
-        base_on_v(3, 1)
+        base_on_v(4, 0)
         quantize_d(*u[6])
         gram(0, 1)
         gram(1, 1)
-        base_on_v(4, 1)
         gram(2, 1)
         square(*u[7])
+        derive(*u[7])
         tanh(*u[8])
-        base_on_s(5, 0)
-        base_matmul(5, 1, "for_s")
+        base_on_s(2, 1)
+        base_matmul(3, 1, "for_s")
         preact(*u[10])
         preact(*u[11])
         finish(0, 1)
         gram(3, 1)
-        derive(*u[7])
-        finish(1, 1)
         quantize_d(*u[7])
-        finish(2, 1)
+        finish(1, 1)
         square(*u[8])
-        base_on_s(5, 1)
-        base_matmul(6, 0, "for_s")
         tanh(*u[9])
-        base_on_s(6, 0)
-        base_matmul(6, 1, "for_s")
+        base_on_s(3, 1)
+        base_matmul(4, 1, "for_s")
+        base_matmul(5, 0, "pre")
+        base_matmul(5, 1, "pre")
         derive(*u[8])
-        finish(3, 1)
+        finish(2, 1)
         quantize_d(*u[8])
         gram(4, 0)
-        square(*u[9])
-        base_on_s(6, 1)
-        base_matmul(7, 0, "for_s")
         gram(4, 1)
+        finish(3, 1)
         gram(5, 0)
+        square(*u[9])
         tanh(*u[10])
-        base_on_s(7, 0)
-        base_matmul(7, 1, "for_s")
+        base_on_s(4, 1)
+        base_matmul(6, 0, "pre")
+        base_matmul(6, 1, "for_s")
         square(*u[10])
         tanh(*u[11])
-        base_on_s(7, 1)
+        base_on_s(5, 0)
+        base_matmul(7, 0, "pre")
+        base_matmul(7, 1, "pre")
         square(*u[11])
+        base_on_s(5, 1)
+        base_on_s(6, 0)
+        base_on_s(6, 1)
+        base_on_s(7, 0)
+        base_on_s(7, 1)
         derive(*u[9])
         finish(4, 0)
         gram(5, 1)
         quantize_d(*u[9])
         finish(4, 1)
         derive(*u[10])
-        finish(5, 0)
         quantize_d(*u[10])
         gram(6, 0)
+        finish(5, 0)
         gram(6, 1)
         derive(*u[11])
         finish(5, 1)
@@ -416,4 +424,4 @@ def tile_twotimehiddentangentkernel_kernel(tc, x, y_bytes, y_scale, wa, wb, b, v
         gram(7, 1)
         finish(6, 1)
         finish(7, 0)
-        finish(7, 1)
+        finish(7, 1, 2)

@@ -21,18 +21,36 @@ PACK = 4
 K_PASS = P * PACK
 BANK = 512
 BLOCK = 256
-BLOCKS = N // BLOCK
 PASSES = F // K_PASS
 PAD = 16
+
 BANKS = {"pre": 4, "for_s": 1, "for_v": 3}
+SQUARE_BUFS = 4
+TANH_BUFS = 2
+D_BUFS = 3
+
+UNITS = [
+    ("a", 0, 0, 256),
+    ("a", 0, 256, 256),
+    ("a", 1, 0, 512),
+    ("b", 0, 0, 512),
+    ("b", 1, 0, 512),
+    ("b", 0, 512, 512),
+    ("b", 1, 512, 512),
+    ("a", 0, 512, 256),
+    ("a", 1, 512, 256),
+    ("a", 0, 768, 256),
+    ("a", 1, 768, 128),
+    ("a", 1, 896, 128),
+]
 
 
 def tile_twotimehiddentangentkernel_kernel(tc, x, y_bytes, y_scale, wa, wb, b, va, vb, out):
     nc = tc.nc
     with ExitStack() as ctx:
         keep = ctx.enter_context(tc.tile_pool(name="keep", bufs=1))
-        work = ctx.enter_context(tc.tile_pool(name="work", bufs=4))
-        psum = ctx.enter_context(tc.psum_pool(name="psum", bufs=4))
+        work = ctx.enter_context(tc.tile_pool(name="work", bufs=SQUARE_BUFS))
+        psum = ctx.enter_context(tc.psum_pool(name="psum", bufs=BANKS["pre"]))
 
         ident = keep.tile([P, P], F32, name="ident")
         make_identity(nc, ident[:])
@@ -44,12 +62,12 @@ def tile_twotimehiddentangentkernel_kernel(tc, x, y_bytes, y_scale, wa, wb, b, v
             scales = keep.tile([P, width], U8, name=name + "_scales", align_bytes=64)
             return codes, scales
 
-        def quantize(dst, col0, grouped):
-            width = grouped.shape[1] // PACK
+        def quantize(operand, col0, values):
+            width = values.shape[1] // PACK
             nc.vector.quantize_mx(
-                out=dst[0][:, col0 : col0 + width].bitcast(FP8X4),
-                scales=dst[1][:, col0 : col0 + width],
-                in_=grouped,
+                out=operand[0][:, col0 : col0 + width].bitcast(FP8X4),
+                scales=operand[1][:, col0 : col0 + width],
+                in_=values,
             )
 
         def mx_matmul(acc, lhs, lhs0, rhs, rhs0, width, start, stop):
@@ -67,26 +85,28 @@ def tile_twotimehiddentangentkernel_kernel(tc, x, y_bytes, y_scale, wa, wb, b, v
         w_mx = {(s, g): mx_tiles("w%s%d" % (s, g), K_PASS) for s in "ab" for g in range(PASSES)}
         d_mx = {(s, g): mx_tiles("d%s%d" % (s, g), N) for s in "ab" for g in range(PASSES)}
         weights = {"a": wa, "b": wb}
-        gains = {"a": va, "b": vb}
-        x_raw, y_raw, w_raw, gain_raw, neg_gain = {}, {}, {}, {}, {}
-        tok_bf, tok_bank, grouped, squares, base_sb = {}, {}, {}, {}, {}
-        pre_banks, tanhs, base_banks, gram_banks = {}, {}, {}, {}
+        y_raw, w_raw, gain_raw, neg_gain = {}, {}, {}, {}
+        tok_rows, tok_banks, tok_grouped, w_grouped = {}, {}, {}, {}
+        pre_banks, tanhs, squares, d_grouped = {}, {}, {}, {}
+        base_banks, base_sb, gram_banks = {}, {}, {}
+
 
         def load_y(blk):
             t = keep.tile([P, 2, D], U8, name="ybytes%d" % blk)
-            nc.sync.dma_start(out=t[:], in_=y_bytes[blk * BLOCK : (blk + 1) * BLOCK, :].rearrange("(a p) k -> p a k", p=P))
+            rows = y_bytes[blk * BLOCK : (blk + 1) * BLOCK, :]
+            nc.sync.dma_start(out=t[:], in_=rows.rearrange("(a p) k -> p a k", p=P))
             y_raw[blk] = t
 
         def load_x(blk):
             t = keep.tile([P, 2, D], BF16, name="xrows%d" % blk)
-            nc.sync.dma_start(out=t[:], in_=x[blk * BLOCK : (blk + 1) * BLOCK, :].rearrange("(p a) k -> p a k", a=2))
-            tok_bf["a", blk] = t
+            rows = x[blk * BLOCK : (blk + 1) * BLOCK, :]
+            nc.sync.dma_start(out=t[:], in_=rows.rearrange("(p a) k -> p a k", a=2))
+            tok_rows["a", blk] = t
 
         def load_w(s, g):
             t = keep.tile([P, PACK, K_PASS], BF16, name="wraw%s%d" % (s, g))
-            nc.sync.dma_start(
-                out=t[:], in_=weights[s][:, g * K_PASS : (g + 1) * K_PASS].rearrange("(p k) c -> p k c", k=PACK)
-            )
+            cols = weights[s][:, g * K_PASS : (g + 1) * K_PASS]
+            nc.sync.dma_start(out=t[:], in_=cols.rearrange("(p k) c -> p k c", k=PACK))
             w_raw[s, g] = t
 
         def load_channels(vec, name):
@@ -112,125 +132,132 @@ def tile_twotimehiddentangentkernel_kernel(tc, x, y_bytes, y_scale, wa, wb, b, v
         load_x(2)
         load_x(3)
 
+
         def negate_gain(s):
             t = keep.tile([P, PASSES, PACK, 2], F32, name="neg_v%s" % s)
             twice = gain_raw[s][:, :, 0:PACK].unsqueeze(3).to_broadcast([P, PASSES, PACK, 2])
             nc.scalar.activation(out=t[:], in_=twice, func=ACT.Copy, scale=-1.0)
             neg_gain[s] = t
 
-        def widen_y(blk, engine_copy):
+        def widen_y(blk):
             t = keep.tile([P, 2, D], BF16, name="ywide%d" % blk)
-            engine_copy(out=t[:], in_=y_raw[blk][:].bitcast(FP8))
-            tok_bf["b", blk] = t
+            nc.vector.tensor_copy(out=t[:], in_=y_raw[blk][:].bitcast(FP8))
+            tok_rows["b", blk] = t
 
         def turn(s, blk):
             tag = "for_v" if s == "b" else "for_s"
-            bank = psum.tile([P, 2, BLOCK], F32, name="turned", tag=tag, bufs=BANKS[tag])
+            bank = psum.tile([P, 2 * BLOCK], F32, name="turned", tag=tag, bufs=BANKS[tag])
+            halves = bank[:].rearrange("p (n u) -> p u n" if s == "b" else "p (u n) -> p u n", u=2)
             for a in range(2):
-                words = tok_bf[s, blk][:, a, :].bitcast(F32)
+                words = tok_rows[s, blk][:, a, :].bitcast(F32)
                 for u in range(2):
-                    nc.tensor.transpose(bank[:, u, a * P : (a + 1) * P], words[:, u : D // 2 : 2], ident[:])
-            tok_bank[s, blk] = bank
+                    nc.tensor.transpose(halves[:, u, a * P : (a + 1) * P], words[:, u : D // 2 : 2], ident[:])
+            tok_banks[s, blk] = bank
 
         def grouped_block(s, blk):
-            if (s, blk // 2) not in grouped:
-                t = keep.tile([P, 2 * BLOCK * PACK], BF16, name="grouped%s%d" % (s, blk // 2), align_bytes=64)
-                grouped[s, blk // 2] = t
-            return grouped[s, blk // 2][:, (blk % 2) * BLOCK * PACK : (blk % 2 + 1) * BLOCK * PACK]
+            pair, second = divmod(blk, 2)
+            if (s, pair) not in tok_grouped:
+                t = keep.tile([P, 2 * BLOCK * PACK], BF16, name="grouped%s%d" % (s, pair), align_bytes=64)
+                tok_grouped[s, pair] = t
+            return tok_grouped[s, pair][:, second * BLOCK * PACK : (second + 1) * BLOCK * PACK]
 
-        def gather_x(blk, engine_copy):
-            t = grouped_block("a", blk)
-            engine_copy(
-                out=t.bitcast(F32).rearrange("p (n u) -> p n u", u=2),
-                in_=tok_bank["a", blk][:].rearrange("p u n -> p n u"),
+        def group_x(blk):
+            nc.scalar.copy(
+                out=grouped_block("a", blk).bitcast(F32).rearrange("p (n u) -> p n u", u=2),
+                in_=tok_banks["a", blk][:].rearrange("p (u n) -> p n u", u=2),
             )
 
         def scale_y(blk):
-            t = grouped_block("b", blk)
-            halves = tok_bank["b", blk][:].rearrange("p u n -> p (u n)").bitcast(BF16)
             nc.vector.tensor_tensor(
-                out=t.rearrange("p (n u e) -> p n u e", u=2, e=2),
-                in0=halves.rearrange("p (u n e) -> p n u e", u=2, e=2),
-                in1=y_gain[:].rearrange("p (u e) -> p u e", e=2).unsqueeze(1).to_broadcast([P, BLOCK, 2, 2]),
+                out=grouped_block("b", blk).rearrange("p (n t) -> p n t", t=PACK),
+                in0=tok_banks["b", blk][:].bitcast(BF16).rearrange("p (n t) -> p n t", t=PACK),
+                in1=y_gain[:].unsqueeze(1).to_broadcast([P, BLOCK, PACK]),
                 op=ALU.mult,
             )
 
-        def quantize_tokens(s, blk):
+        def quantize_block(s, blk):
             quantize(tok_mx[s], blk * BLOCK, grouped_block(s, blk))
 
         def quantize_pair(s, pair):
-            quantize(tok_mx[s], pair * 2 * BLOCK, grouped[s, pair][:])
+            quantize(tok_mx[s], pair * 2 * BLOCK, tok_grouped[s, pair][:])
 
         def group_w(s, g, copies):
             share = PACK // len(copies)
             src = w_raw[s, g][:].rearrange("p k (h l j) -> p h j l k", l=2, j=PACK)
-            for i, engine_copy in enumerate(copies):
-                t = keep.tile([P, share * K_PASS], BF16, name="wgrouped%s%d_%d" % (s, g, i), align_bytes=64)
+            for part, engine_copy in enumerate(copies):
+                t = keep.tile([P, share * K_PASS], BF16, name="wgrouped%s%d_%d" % (s, g, part), align_bytes=64)
                 engine_copy(
                     out=t[:].rearrange("p (j h l k) -> p h j l k", j=share, l=2, k=PACK),
-                    in_=src[:, :, i * share : (i + 1) * share],
+                    in_=src[:, :, part * share : (part + 1) * share],
                 )
-                grouped["w", s, g, i] = t
+                w_grouped[s, g, part] = t
 
         def quantize_w(s, g, part=0, parts=1):
-            quantize(w_mx[s, g], part * K_PASS // parts, grouped["w", s, g, part][:])
+            quantize(w_mx[s, g], part * K_PASS // parts, w_grouped[s, g, part][:])
 
-        def preact(s, g, col0, width):
+
+        def preact(unit):
+            s, g, col0, width = UNITS[unit]
             per_bank = BANK // width
             views = []
             for j0 in range(0, PACK, per_bank):
                 bank = psum.tile([P, per_bank, width], F32, name="pre", tag="pre", bufs=BANKS["pre"])
-                for i in range(min(per_bank, PACK)):
-                    mx_matmul(bank[:, i, :], w_mx[s, g], (j0 + i) * P, tok_mx[s], col0, width, True, True)
-                    views.append(bank[:, i, :])
-            pre_banks[s, g, col0] = views
+                for slot in range(per_bank):
+                    mx_matmul(bank[:, slot, :], w_mx[s, g], (j0 + slot) * P, tok_mx[s], col0, width, True, True)
+                    views.append(bank[:, slot, :])
+            pre_banks[unit] = views
 
-        def tanh(s, g, col0, width):
-            planes = work.tile([P, PACK, width], F32, name="tanh_planes", tag="tanh_planes", bufs=2)
+        def tanh(unit):
+            g, width = UNITS[unit][1], UNITS[unit][3]
+            planes = work.tile([P, PACK, width], F32, name="tanh_planes", tag="tanh_planes", bufs=TANH_BUFS)
             for j in range(PACK):
                 nc.scalar.activation(
                     out=planes[:, j, :].rearrange("p (c i) -> p c i", i=2),
-                    in_=pre_banks[s, g, col0][j].rearrange("p (i c) -> p c i", i=2),
+                    in_=pre_banks[unit][j].rearrange("p (i c) -> p c i", i=2),
                     func=ACT.Tanh,
                     bias=bias[:, g, j : j + 1],
                 )
-            tanhs[s, g, col0] = planes
+            tanhs[unit] = planes
 
-        def square(s, g, col0, width):
-            sq = work.tile([P, width * PACK], F32, name="squares", tag="squares")
+        def square(unit):
+            width = UNITS[unit][3]
+            t = work.tile([P, width * PACK], F32, name="squares", tag="squares")
             nc.scalar.activation(
-                out=sq[:].rearrange("p (c j i) -> p c j i", i=2, j=PACK),
-                in_=tanhs[s, g, col0][:].rearrange("p j (c i) -> p c j i", i=2),
+                out=t[:].rearrange("p (c j i) -> p c j i", i=2, j=PACK),
+                in_=tanhs[unit][:].rearrange("p j (c i) -> p c j i", i=2),
                 func=ACT.Square,
             )
-            squares[s, g, col0] = sq
+            squares[unit] = t
 
-        def derive(s, g, col0, width):
-            t = work.tile([P, width * PACK], BF16, name="dgrouped", tag="dgrouped", bufs=3, align_bytes=64)
+        def derive(unit):
+            s, g, width = UNITS[unit][0], UNITS[unit][1], UNITS[unit][3]
+            t = work.tile([P, width * PACK], BF16, name="dgrouped", tag="dgrouped", bufs=D_BUFS, align_bytes=64)
             nc.vector.scalar_tensor_tensor(
                 out=t[:].rearrange("p (i c j) -> p c j i", i=2, j=PACK),
-                in0=squares[s, g, col0][:].rearrange("p (c j i) -> p c j i", i=2, j=PACK),
+                in0=squares[unit][:].rearrange("p (c j i) -> p c j i", i=2, j=PACK),
                 scalar=1.0,
                 in1=neg_gain[s][:, g].unsqueeze(1).to_broadcast([P, width // 2, PACK, 2]),
                 op0=ALU.subtract,
                 op1=ALU.mult,
             )
-            grouped["d", s, g, col0] = t
+            d_grouped[unit] = t
 
-        def quantize_d(s, g, col0, width):
-            quantize(d_mx[s, g], col0, grouped["d", s, g, col0][:])
+        def quantize_d(unit):
+            s, g, col0 = UNITS[unit][0:3]
+            quantize(d_mx[s, g], col0, d_grouped[unit][:])
+
 
         def base_matmul(tile, half, tag):
             bank = psum.tile([P, BANK], F32, name="base_acc", tag=tag, bufs=BANKS[tag])
             mx_matmul(bank[:], tok_mx["a"], tile * P, tok_mx["b"], half * BANK, BANK, True, True)
             base_banks[tile, half] = bank
 
-        def base_on_s(tile, half):
+        def base_on_scalar(tile, half):
             t = keep.tile([P, BANK], F32, name="base%d_%d" % (tile, half))
             nc.scalar.activation(out=t[:], in_=base_banks[tile, half][:], func=ACT.Copy, scale=1.0 / math.sqrt(D))
             base_sb[tile, half] = t
 
-        def base_on_v(tile, half):
+        def base_on_vector(tile, half):
             t = keep.tile([P, BANK], F32, name="base%d_%d" % (tile, half))
             nc.vector.tensor_scalar(
                 out=t[:], in0=base_banks[tile, half][:], scalar1=1.0 / math.sqrt(D), scalar2=None, op0=ALU.mult
@@ -243,12 +270,12 @@ def tile_twotimehiddentangentkernel_kernel(tc, x, y_bytes, y_scale, wa, wb, b, v
                 mx_matmul(bank[:], d_mx["a", g], tile * P, d_mx["b", g], half * BANK, BANK, g == 0, g == PASSES - 1)
             gram_banks[tile, half] = bank
 
-        def finish(tile, half, pieces=1):
+        def finish(tile, half, parts=1):
             blk, a = divmod(tile, 2)
-            width = BANK // pieces
-            for i in range(pieces):
-                cols = slice(i * width, (i + 1) * width)
-                t = keep.tile([P, width], F32, name="out%d_%d_%d" % (tile, half, i))
+            width = BANK // parts
+            for part in range(parts):
+                cols = slice(part * width, (part + 1) * width)
+                t = keep.tile([P, width], F32, name="out%d_%d_%d" % (tile, half, part))
                 nc.vector.scalar_tensor_tensor(
                     out=t[:],
                     in0=gram_banks[tile, half][:, cols],
@@ -257,171 +284,182 @@ def tile_twotimehiddentangentkernel_kernel(tc, x, y_bytes, y_scale, wa, wb, b, v
                     op0=ALU.mult,
                     op1=ALU.mult,
                 )
-                m0 = half * BANK + i * width
+                m0 = half * BANK + part * width
                 rows = out[blk * BLOCK : (blk + 1) * BLOCK, m0 : m0 + width]
                 nc.sync.dma_start(out=rows.rearrange("(p a) m -> p a m", a=2)[:, a, :], in_=t[:])
 
-        on_s, on_v = nc.scalar.copy, nc.vector.tensor_copy
-        u = [("a", 0, 0, 256), ("a", 0, 256, 256), ("a", 1, 0, 512), ("b", 0, 0, 512), ("b", 1, 0, 512),
-             ("b", 0, 512, 512), ("b", 1, 512, 512), ("a", 0, 512, 256), ("a", 1, 512, 256), ("a", 0, 768, 256),
-             ("a", 1, 768, 128), ("a", 1, 896, 128)]
+        on_vector, on_scalar = nc.vector.tensor_copy, nc.scalar.copy
+
         turn("a", 0)
-        widen_y(0, on_v)
-        gather_x(0, on_s)
-        group_w("a", 0, [on_v, on_s])
-        quantize_tokens("a", 0)
-        quantize_w("a", 0, 0, 2)
+        widen_y(0)
+        group_x(0)
+        group_w("a", 0, [on_vector, on_scalar])
+        quantize_block("a", 0)
+        quantize_w("a", 0, part=0, parts=2)
         turn("a", 1)
-        widen_y(1, on_v)
-        quantize_w("a", 0, 1, 2)
-        gather_x(1, on_s)
-        preact(*u[0])
+        widen_y(1)
+        quantize_w("a", 0, part=1, parts=2)
+        group_x(1)
+        preact(0)
         turn("b", 0)
-        group_w("a", 1, [on_v])
-        quantize_tokens("a", 1)
-        tanh(*u[0])
-        preact(*u[1])
+        group_w("a", 1, [on_vector])
+        quantize_block("a", 1)
+
+        tanh(0)
+        preact(1)
         turn("b", 1)
-        scale_y(0)
         quantize_w("a", 1)
         negate_gain("a")
-        square(*u[0])
-        tanh(*u[1])
-        preact(*u[2])
-        scale_y(1)
-        group_w("b", 0, [on_v])
-        quantize_pair("b", 0)
-        base_matmul(0, 0, "for_s")
-        negate_gain("b")
-        square(*u[1])
-        tanh(*u[2])
-        derive(*u[0])
+        square(0)
+
+        tanh(1)
+        preact(2)
+        turn("a", 2)
+        group_w("b", 0, [on_vector])
+        scale_y(0)
         quantize_w("b", 0)
-        base_on_s(0, 0)
-        preact(*u[3])
-        base_matmul(1, 0, "for_s")
-        group_w("b", 1, [on_v])
-        quantize_d(*u[0])
-        derive(*u[1])
-        quantize_w("b", 1)
-        quantize_d(*u[1])
-        widen_y(2, on_v)
-        widen_y(3, on_v)
-        square(*u[2])
-        tanh(*u[3])
-        base_on_s(1, 0)
-        preact(*u[4])
+        scale_y(1)
+        negate_gain("b")
+        square(1)
+
+        tanh(2)
+        widen_y(2)
+        quantize_pair("b", 0)
+        group_x(2)
+        preact(3)
+        base_matmul(0, 0, "for_s")
+        widen_y(3)
         turn("b", 2)
         turn("b", 3)
-        turn("a", 2)
+        derive(0)
+        group_w("b", 1, [on_vector])
+        quantize_d(0)
+        derive(1)
+        quantize_w("b", 1)
+        quantize_d(1)
+        square(2)
+
+        tanh(3)
+        base_on_scalar(0, 0)
+        preact(4)
+        base_matmul(1, 0, "for_s")
         base_matmul(2, 0, "for_v")
-        derive(*u[2])
+        derive(2)
         scale_y(2)
         base_matmul(3, 0, "for_v")
         scale_y(3)
-        quantize_d(*u[2])
+        quantize_d(2)
         quantize_pair("b", 1)
-        square(*u[3])
-        tanh(*u[4])
-        gather_x(2, on_s)
+        square(3)
+
+        tanh(4)
+        base_on_scalar(1, 0)
         turn("a", 3)
-        preact(*u[5])
-        derive(*u[3])
-        base_on_v(2, 0)
-        quantize_d(*u[3])
-        square(*u[4])
-        tanh(*u[5])
-        gather_x(3, on_s)
-        preact(*u[6])
+        preact(5)
+        derive(3)
+        base_on_vector(2, 0)
+        quantize_d(3)
+        square(4)
+
+        tanh(5)
+        group_x(3)
+        preact(6)
         base_matmul(0, 1, "for_s")
-        derive(*u[4])
-        base_on_v(3, 0)
-        quantize_d(*u[4])
+        derive(4)
+        base_on_vector(3, 0)
+        quantize_d(4)
         gram(0, 0)
         gram(1, 0)
         gram(2, 0)
         quantize_pair("a", 1)
-        square(*u[5])
+        square(5)
         finish(0, 0)
         gram(3, 0)
         finish(1, 0)
-        tanh(*u[6])
-        base_on_s(0, 1)
-        preact(*u[7])
+
+        tanh(6)
+        base_on_scalar(0, 1)
+        preact(7)
         base_matmul(1, 1, "for_s")
-        preact(*u[8])
-        derive(*u[5])
+        preact(8)
+        derive(5)
         finish(2, 0)
         base_matmul(4, 0, "for_v")
-        quantize_d(*u[5])
+        quantize_d(5)
         finish(3, 0)
-        square(*u[6])
-        tanh(*u[7])
-        base_on_s(1, 1)
+        square(6)
+
+        tanh(7)
+        base_on_scalar(1, 1)
         base_matmul(2, 1, "for_s")
-        preact(*u[9])
-        derive(*u[6])
-        base_on_v(4, 0)
-        quantize_d(*u[6])
+        preact(9)
+        derive(6)
+        base_on_vector(4, 0)
+        quantize_d(6)
         gram(0, 1)
         gram(1, 1)
         gram(2, 1)
-        square(*u[7])
-        derive(*u[7])
-        tanh(*u[8])
-        base_on_s(2, 1)
+        square(7)
+        derive(7)
+
+        tanh(8)
+        base_on_scalar(2, 1)
         base_matmul(3, 1, "for_s")
-        preact(*u[10])
-        preact(*u[11])
+        preact(10)
+        preact(11)
         finish(0, 1)
         gram(3, 1)
-        quantize_d(*u[7])
+        quantize_d(7)
         finish(1, 1)
-        square(*u[8])
-        tanh(*u[9])
-        base_on_s(3, 1)
+        square(8)
+
+        tanh(9)
+        base_on_scalar(3, 1)
         base_matmul(4, 1, "for_s")
         base_matmul(5, 0, "pre")
         base_matmul(5, 1, "pre")
-        derive(*u[8])
+        derive(8)
         finish(2, 1)
-        quantize_d(*u[8])
+        quantize_d(8)
         gram(4, 0)
         gram(4, 1)
         finish(3, 1)
         gram(5, 0)
-        square(*u[9])
-        tanh(*u[10])
-        base_on_s(4, 1)
+        square(9)
+
+        tanh(10)
+        base_on_scalar(4, 1)
         base_matmul(6, 0, "pre")
         base_matmul(6, 1, "for_s")
-        square(*u[10])
-        tanh(*u[11])
-        base_on_s(5, 0)
+        square(10)
+
+        tanh(11)
+        base_on_scalar(5, 0)
         base_matmul(7, 0, "pre")
         base_matmul(7, 1, "pre")
-        square(*u[11])
-        base_on_s(5, 1)
-        base_on_s(6, 0)
-        base_on_s(6, 1)
-        base_on_s(7, 0)
-        base_on_s(7, 1)
-        derive(*u[9])
+        square(11)
+        base_on_scalar(5, 1)
+        base_on_scalar(6, 0)
+        base_on_scalar(6, 1)
+        base_on_scalar(7, 0)
+        base_on_scalar(7, 1)
+
+        derive(9)
         finish(4, 0)
         gram(5, 1)
-        quantize_d(*u[9])
+        quantize_d(9)
         finish(4, 1)
-        derive(*u[10])
-        quantize_d(*u[10])
+        derive(10)
+        quantize_d(10)
         gram(6, 0)
         finish(5, 0)
         gram(6, 1)
-        derive(*u[11])
+        derive(11)
         finish(5, 1)
-        quantize_d(*u[11])
+        quantize_d(11)
         gram(7, 0)
         finish(6, 0)
         gram(7, 1)
         finish(6, 1)
         finish(7, 0)
-        finish(7, 1, 2)
+        finish(7, 1, parts=2)

import math
from contextlib import ExitStack

import concourse.mybir as mybir
from concourse.masks import make_identity

N, M, D, F = 1024, 1024, 512, 1024
FLOPS = 2 * N * D * F + 2 * M * D * F + 2 * N * M * D + 2 * N * M * F

F32 = mybir.dt.float32
BF16 = mybir.dt.bfloat16
U32 = mybir.dt.uint32
U8 = mybir.dt.uint8
FP8 = mybir.dt.float8_e4m3fn
FP8X4 = mybir.dt.float8_e4m3fn_x4
ACT = mybir.ActivationFunctionType
ALU = mybir.AluOpType

P = 128
PACK = 4
K_PASS = P * PACK
BANK = 512
BLOCK = 256
PASSES = F // K_PASS
PAD = 16

BANKS = {"pre": 4, "for_s": 1, "for_v": 3}
SQUARE_BUFS = 4
TANH_BUFS = 2
D_BUFS = 3

UNITS = [
    ("a", 0, 0, 256),
    ("a", 0, 256, 256),
    ("a", 1, 0, 512),
    ("b", 0, 0, 512),
    ("b", 1, 0, 512),
    ("b", 0, 512, 512),
    ("b", 1, 512, 512),
    ("a", 0, 512, 256),
    ("a", 1, 512, 256),
    ("a", 0, 768, 256),
    ("a", 1, 768, 128),
    ("a", 1, 896, 128),
]


def tile_twotimehiddentangentkernel_kernel(tc, x, y_bytes, y_scale, wa, wb, b, va, vb, out):
    nc = tc.nc
    with ExitStack() as ctx:
        keep = ctx.enter_context(tc.tile_pool(name="keep", bufs=1))
        work = ctx.enter_context(tc.tile_pool(name="work", bufs=SQUARE_BUFS))
        psum = ctx.enter_context(tc.psum_pool(name="psum", bufs=BANKS["pre"]))

        ident = keep.tile([P, P], F32, name="ident")
        make_identity(nc, ident[:])

        ctx.enter_context(tc.manual_schedule())

        def mx_tiles(name, width):
            codes = keep.tile([P, width], U32, name=name + "_codes", align_bytes=64)
            scales = keep.tile([P, width], U8, name=name + "_scales", align_bytes=64)
            return codes, scales

        def quantize(operand, col0, values):
            width = values.shape[1] // PACK
            nc.vector.quantize_mx(
                out=operand[0][:, col0 : col0 + width].bitcast(FP8X4),
                scales=operand[1][:, col0 : col0 + width],
                in_=values,
            )

        def mx_matmul(acc, lhs, lhs0, rhs, rhs0, width, start, stop):
            nc.tensor.matmul_mx(
                out=acc,
                lhsT=lhs[0][:, lhs0 : lhs0 + P].bitcast(FP8X4),
                lhsT_scale=lhs[1][:, lhs0 : lhs0 + P],
                rhs=rhs[0][:, rhs0 : rhs0 + width].bitcast(FP8X4),
                rhs_scale=rhs[1][:, rhs0 : rhs0 + width],
                start=start,
                stop=stop,
            )

        tok_mx = {"a": mx_tiles("x", N), "b": mx_tiles("y", M)}
        w_mx = {(s, g): mx_tiles("w%s%d" % (s, g), K_PASS) for s in "ab" for g in range(PASSES)}
        d_mx = {(s, g): mx_tiles("d%s%d" % (s, g), N) for s in "ab" for g in range(PASSES)}
        weights = {"a": wa, "b": wb}
        y_raw, w_raw, gain_raw, neg_gain = {}, {}, {}, {}
        tok_rows, tok_banks, tok_grouped, w_grouped = {}, {}, {}, {}
        pre_banks, tanhs, squares, d_grouped = {}, {}, {}, {}
        base_banks, base_sb, gram_banks = {}, {}, {}


        def load_y(blk):
            t = keep.tile([P, 2, D], U8, name="ybytes%d" % blk)
            rows = y_bytes[blk * BLOCK : (blk + 1) * BLOCK, :]
            nc.sync.dma_start(out=t[:], in_=rows.rearrange("(a p) k -> p a k", p=P))
            y_raw[blk] = t

        def load_x(blk):
            t = keep.tile([P, 2, D], BF16, name="xrows%d" % blk)
            rows = x[blk * BLOCK : (blk + 1) * BLOCK, :]
            nc.sync.dma_start(out=t[:], in_=rows.rearrange("(p a) k -> p a k", a=2))
            tok_rows["a", blk] = t

        def load_w(s, g):
            t = keep.tile([P, PACK, K_PASS], BF16, name="wraw%s%d" % (s, g))
            cols = weights[s][:, g * K_PASS : (g + 1) * K_PASS]
            nc.sync.dma_start(out=t[:], in_=cols.rearrange("(p k) c -> p k c", k=PACK))
            w_raw[s, g] = t

        def load_channels(vec, name):
            t = keep.tile([P, PASSES, PAD], BF16, name=name)
            nc.sync.dma_start(out=t[:, :, 0:PACK], in_=vec.rearrange("(g p j) -> p g j", p=P, j=PACK))
            return t

        load_x(0)
        load_y(0)
        load_w("a", 0)
        load_x(1)
        load_y(1)
        bias = load_channels(b, "bias")
        gain_raw["a"] = load_channels(va, "va_raw")
        load_w("a", 1)
        y_gain = keep.tile([P, PACK], F32, name="y_gain")
        nc.sync.dma_start(out=y_gain[:], in_=y_scale.rearrange("o (p t) -> p (o t)", t=PACK))
        load_w("b", 0)
        gain_raw["b"] = load_channels(vb, "vb_raw")
        load_y(2)
        load_y(3)
        load_w("b", 1)
        load_x(2)
        load_x(3)


        def negate_gain(s):
            t = keep.tile([P, PASSES, PACK, 2], F32, name="neg_v%s" % s)
            twice = gain_raw[s][:, :, 0:PACK].unsqueeze(3).to_broadcast([P, PASSES, PACK, 2])
            nc.scalar.activation(out=t[:], in_=twice, func=ACT.Copy, scale=-1.0)
            neg_gain[s] = t

        def widen_y(blk):
            t = keep.tile([P, 2, D], BF16, name="ywide%d" % blk)
            nc.vector.tensor_copy(out=t[:], in_=y_raw[blk][:].bitcast(FP8))
            tok_rows["b", blk] = t

        def turn(s, blk):
            tag = "for_v" if s == "b" else "for_s"
            bank = psum.tile([P, 2 * BLOCK], F32, name="turned", tag=tag, bufs=BANKS[tag])
            halves = bank[:].rearrange("p (n u) -> p u n" if s == "b" else "p (u n) -> p u n", u=2)
            for a in range(2):
                words = tok_rows[s, blk][:, a, :].bitcast(F32)
                for u in range(2):
                    nc.tensor.transpose(halves[:, u, a * P : (a + 1) * P], words[:, u : D // 2 : 2], ident[:])
            tok_banks[s, blk] = bank

        def grouped_block(s, blk):
            pair, second = divmod(blk, 2)
            if (s, pair) not in tok_grouped:
                t = keep.tile([P, 2 * BLOCK * PACK], BF16, name="grouped%s%d" % (s, pair), align_bytes=64)
                tok_grouped[s, pair] = t
            return tok_grouped[s, pair][:, second * BLOCK * PACK : (second + 1) * BLOCK * PACK]

        def group_x(blk):
            nc.scalar.copy(
                out=grouped_block("a", blk).bitcast(F32).rearrange("p (n u) -> p n u", u=2),
                in_=tok_banks["a", blk][:].rearrange("p (u n) -> p n u", u=2),
            )

        def scale_y(blk):
            nc.vector.tensor_tensor(
                out=grouped_block("b", blk).rearrange("p (n t) -> p n t", t=PACK),
                in0=tok_banks["b", blk][:].bitcast(BF16).rearrange("p (n t) -> p n t", t=PACK),
                in1=y_gain[:].unsqueeze(1).to_broadcast([P, BLOCK, PACK]),
                op=ALU.mult,
            )

        def quantize_block(s, blk):
            quantize(tok_mx[s], blk * BLOCK, grouped_block(s, blk))

        def quantize_pair(s, pair):
            quantize(tok_mx[s], pair * 2 * BLOCK, tok_grouped[s, pair][:])

        def group_w(s, g, copies):
            share = PACK // len(copies)
            src = w_raw[s, g][:].rearrange("p k (h l j) -> p h j l k", l=2, j=PACK)
            for part, engine_copy in enumerate(copies):
                t = keep.tile([P, share * K_PASS], BF16, name="wgrouped%s%d_%d" % (s, g, part), align_bytes=64)
                engine_copy(
                    out=t[:].rearrange("p (j h l k) -> p h j l k", j=share, l=2, k=PACK),
                    in_=src[:, :, part * share : (part + 1) * share],
                )
                w_grouped[s, g, part] = t

        def quantize_w(s, g, part=0, parts=1):
            quantize(w_mx[s, g], part * K_PASS // parts, w_grouped[s, g, part][:])


        def preact(unit):
            s, g, col0, width = UNITS[unit]
            per_bank = BANK // width
            views = []
            for j0 in range(0, PACK, per_bank):
                bank = psum.tile([P, per_bank, width], F32, name="pre", tag="pre", bufs=BANKS["pre"])
                for slot in range(per_bank):
                    mx_matmul(bank[:, slot, :], w_mx[s, g], (j0 + slot) * P, tok_mx[s], col0, width, True, True)
                    views.append(bank[:, slot, :])
            pre_banks[unit] = views

        def tanh(unit):
            g, width = UNITS[unit][1], UNITS[unit][3]
            planes = work.tile([P, PACK, width], F32, name="tanh_planes", tag="tanh_planes", bufs=TANH_BUFS)
            for j in range(PACK):
                nc.scalar.activation(
                    out=planes[:, j, :].rearrange("p (c i) -> p c i", i=2),
                    in_=pre_banks[unit][j].rearrange("p (i c) -> p c i", i=2),
                    func=ACT.Tanh,
                    bias=bias[:, g, j : j + 1],
                )
            tanhs[unit] = planes

        def square(unit):
            width = UNITS[unit][3]
            t = work.tile([P, width * PACK], F32, name="squares", tag="squares")
            nc.scalar.activation(
                out=t[:].rearrange("p (c j i) -> p c j i", i=2, j=PACK),
                in_=tanhs[unit][:].rearrange("p j (c i) -> p c j i", i=2),
                func=ACT.Square,
            )
            squares[unit] = t

        def derive(unit):
            s, g, width = UNITS[unit][0], UNITS[unit][1], UNITS[unit][3]
            t = work.tile([P, width * PACK], BF16, name="dgrouped", tag="dgrouped", bufs=D_BUFS, align_bytes=64)
            nc.vector.scalar_tensor_tensor(
                out=t[:].rearrange("p (i c j) -> p c j i", i=2, j=PACK),
                in0=squares[unit][:].rearrange("p (c j i) -> p c j i", i=2, j=PACK),
                scalar=1.0,
                in1=neg_gain[s][:, g].unsqueeze(1).to_broadcast([P, width // 2, PACK, 2]),
                op0=ALU.subtract,
                op1=ALU.mult,
            )
            d_grouped[unit] = t

        def quantize_d(unit):
            s, g, col0 = UNITS[unit][0:3]
            quantize(d_mx[s, g], col0, d_grouped[unit][:])


        def base_matmul(tile, half, tag):
            bank = psum.tile([P, BANK], F32, name="base_acc", tag=tag, bufs=BANKS[tag])
            mx_matmul(bank[:], tok_mx["a"], tile * P, tok_mx["b"], half * BANK, BANK, True, True)
            base_banks[tile, half] = bank

        def base_on_scalar(tile, half):
            t = keep.tile([P, BANK], F32, name="base%d_%d" % (tile, half))
            nc.scalar.activation(out=t[:], in_=base_banks[tile, half][:], func=ACT.Copy, scale=1.0 / math.sqrt(D))
            base_sb[tile, half] = t

        def base_on_vector(tile, half):
            t = keep.tile([P, BANK], F32, name="base%d_%d" % (tile, half))
            nc.vector.tensor_scalar(
                out=t[:], in0=base_banks[tile, half][:], scalar1=1.0 / math.sqrt(D), scalar2=None, op0=ALU.mult
            )
            base_sb[tile, half] = t

        def gram(tile, half):
            bank = psum.tile([P, BANK], F32, name="gram_acc", tag="for_v", bufs=BANKS["for_v"])
            for g in range(PASSES):
                mx_matmul(bank[:], d_mx["a", g], tile * P, d_mx["b", g], half * BANK, BANK, g == 0, g == PASSES - 1)
            gram_banks[tile, half] = bank

        def finish(tile, half, parts=1):
            blk, a = divmod(tile, 2)
            width = BANK // parts
            for part in range(parts):
                cols = slice(part * width, (part + 1) * width)
                t = keep.tile([P, width], F32, name="out%d_%d_%d" % (tile, half, part))
                nc.vector.scalar_tensor_tensor(
                    out=t[:],
                    in0=gram_banks[tile, half][:, cols],
                    scalar=1.0 / math.sqrt(F),
                    in1=base_sb[tile, half][:, cols],
                    op0=ALU.mult,
                    op1=ALU.mult,
                )
                m0 = half * BANK + part * width
                rows = out[blk * BLOCK : (blk + 1) * BLOCK, m0 : m0 + width]
                nc.sync.dma_start(out=rows.rearrange("(p a) m -> p a m", a=2)[:, a, :], in_=t[:])

        on_vector, on_scalar = nc.vector.tensor_copy, nc.scalar.copy

        turn("a", 0)
        widen_y(0)
        group_x(0)
        group_w("a", 0, [on_vector, on_scalar])
        quantize_block("a", 0)
        quantize_w("a", 0, part=0, parts=2)
        turn("a", 1)
        widen_y(1)
        quantize_w("a", 0, part=1, parts=2)
        group_x(1)
        preact(0)
        turn("b", 0)
        group_w("a", 1, [on_vector])
        quantize_block("a", 1)

        tanh(0)
        preact(1)
        turn("b", 1)
        quantize_w("a", 1)
        negate_gain("a")
        square(0)

        tanh(1)
        preact(2)
        turn("a", 2)
        group_w("b", 0, [on_vector])
        scale_y(0)
        quantize_w("b", 0)
        scale_y(1)
        negate_gain("b")
        square(1)

        tanh(2)
        widen_y(2)
        quantize_pair("b", 0)
        group_x(2)
        preact(3)
        base_matmul(0, 0, "for_s")
        widen_y(3)
        turn("b", 2)
        turn("b", 3)
        derive(0)
        group_w("b", 1, [on_vector])
        quantize_d(0)
        derive(1)
        quantize_w("b", 1)
        quantize_d(1)
        square(2)

        tanh(3)
        base_on_scalar(0, 0)
        preact(4)
        base_matmul(1, 0, "for_s")
        base_matmul(2, 0, "for_v")
        derive(2)
        scale_y(2)
        base_matmul(3, 0, "for_v")
        scale_y(3)
        quantize_d(2)
        quantize_pair("b", 1)
        square(3)

        tanh(4)
        base_on_scalar(1, 0)
        turn("a", 3)
        preact(5)
        derive(3)
        base_on_vector(2, 0)
        quantize_d(3)
        square(4)

        tanh(5)
        group_x(3)
        preact(6)
        base_matmul(0, 1, "for_s")
        derive(4)
        base_on_vector(3, 0)
        quantize_d(4)
        gram(0, 0)
        gram(1, 0)
        gram(2, 0)
        quantize_pair("a", 1)
        square(5)
        finish(0, 0)
        gram(3, 0)
        finish(1, 0)

        tanh(6)
        base_on_scalar(0, 1)
        preact(7)
        base_matmul(1, 1, "for_s")
        preact(8)
        derive(5)
        finish(2, 0)
        base_matmul(4, 0, "for_v")
        quantize_d(5)
        finish(3, 0)
        square(6)

        tanh(7)
        base_on_scalar(1, 1)
        base_matmul(2, 1, "for_s")
        preact(9)
        derive(6)
        base_on_vector(4, 0)
        quantize_d(6)
        gram(0, 1)
        gram(1, 1)
        gram(2, 1)
        square(7)
        derive(7)

        tanh(8)
        base_on_scalar(2, 1)
        base_matmul(3, 1, "for_s")
        preact(10)
        preact(11)
        finish(0, 1)
        gram(3, 1)
        quantize_d(7)
        finish(1, 1)
        square(8)

        tanh(9)
        base_on_scalar(3, 1)
        base_matmul(4, 1, "for_s")
        base_matmul(5, 0, "pre")
        base_matmul(5, 1, "pre")
        derive(8)
        finish(2, 1)
        quantize_d(8)
        gram(4, 0)
        gram(4, 1)
        finish(3, 1)
        gram(5, 0)
        square(9)

        tanh(10)
        base_on_scalar(4, 1)
        base_matmul(6, 0, "pre")
        base_matmul(6, 1, "for_s")
        square(10)

        tanh(11)
        base_on_scalar(5, 0)
        base_matmul(7, 0, "pre")
        base_matmul(7, 1, "pre")
        square(11)
        base_on_scalar(5, 1)
        base_on_scalar(6, 0)
        base_on_scalar(6, 1)
        base_on_scalar(7, 0)
        base_on_scalar(7, 1)

        derive(9)
        finish(4, 0)
        gram(5, 1)
        quantize_d(9)
        finish(4, 1)
        derive(10)
        quantize_d(10)
        gram(6, 0)
        finish(5, 0)
        gram(6, 1)
        derive(11)
        finish(5, 1)
        quantize_d(11)
        gram(7, 0)
        finish(6, 0)
        gram(7, 1)
        finish(6, 1)
        finish(7, 0)
        finish(7, 1, parts=2)
